import numpy as np
import ml_dtypes


def mxq(x, axis, fmt="e4m3"):
    dtype, down = {"e4m3": (ml_dtypes.float8_e4m3fn, 7), "e5m2": (ml_dtypes.float8_e5m2, 14)}[fmt]
    v = np.moveaxis(np.asarray(x, np.float32).astype(ml_dtypes.bfloat16).astype(np.float64), axis, -1)
    blocks = v.reshape(v.shape[:-1] + (-1, 32))
    amax = np.abs(blocks).max(-1, keepdims=True)
    byte = np.maximum(np.where(amax > 0, np.frexp(amax)[1] - 1 + 127, 0) - down, 1)
    scale = np.exp2(byte - 127.0)
    codes = (blocks / scale).astype(np.float32).astype(dtype).astype(np.float64)
    return np.moveaxis((codes * scale).reshape(v.shape), -1, axis)


WIDE = False


def mx_kscale(k):
    if not WIDE:
        return np.ones(k)
    levels = np.array([10, -10, 5, -5, 0])
    if k % 512:
        return np.exp2(np.random.permutation(np.resize(levels, k // 32))).repeat(32)
    a = np.empty((k // 512, 16))
    for p in range(k // 512):
        a[p, :8] = np.random.permutation(np.resize(levels, 8))
        for g in range(8):
            far = levels[np.abs(levels - a[p, g]) >= 10]
            a[p, g + 8] = far[np.random.randint(len(far))]
    return np.exp2(a.ravel()).repeat(32)


BF16 = ml_dtypes.bfloat16


def bf(x):
    return np.asarray(x, np.float32).astype(BF16)


def f64(x):
    return np.asarray(x).astype(np.float64)


N, G, S = 1024, 4, 512
D = G * S


def draw0():
    s, t2 = mx_kscale(S), mx_kscale(S)
    root_s = np.sqrt(S)
    return {
        "x": bf((np.random.standard_normal((N, G, S)) * s).reshape(N, D)),
        "t": bf(np.random.standard_normal((N, D))),
        "lblk": bf(np.random.standard_normal((G, S, S)) / root_s / s[:, None]),
        "rblk": bf(2.0 * np.random.standard_normal((G, S, S)) / root_s / t2[:, None]),
        "kern": bf(1.0 + 0.1 * np.random.standard_normal((G, S))),
        "b": bf(0.4 * np.random.standard_normal((G, S))),
        "gain": bf((1.0 + 0.1 * np.random.standard_normal((G, S))) * t2),
    }


def gelu_tanh(a):
    c = np.sqrt(2.0 / np.pi)
    return 0.5 * a * (1.0 + np.tanh(c * (a + 0.044715 * (a * a * a))))


def block_product(h, blocks):
    hq = mxq(h.transpose(1, 0, 2), 2, "e4m3")
    bq = mxq(blocks, 1, "e4m3")
    return (hq @ bq).transpose(1, 0, 2)


def stride_permute(u):
    n, g, s = u.shape
    pf = u.transpose(0, 2, 1).reshape(n, g * s)
    return pf.reshape(n, g, s)


def stride_unpermute(v):
    n, g, s = v.shape
    vf = v.reshape(n, g * s)
    w = vf.reshape(n, s, g).transpose(0, 2, 1)
    return w.reshape(n, g * s)


def core(x, t, lblk, rblk, kern, b, gain):
    x, t, lblk, rblk, kern, b, gain = f64(x), f64(t), f64(lblk), f64(rblk), f64(kern), f64(b), f64(gain)
    n = x.shape[0]
    g, s = kern.shape

    xg = x.reshape(n, g, s)
    u = block_product(xg, lblk)

    p = stride_permute(u)

    a = kern[None, :, :] * p + b[None, :, :]

    m = gain[None, :, :] * gelu_tanh(a)

    v = block_product(m, rblk)

    y = stride_unpermute(v)

    return y * (1.0 / (1.0 + np.exp(-t)))


def e4m3fn_bytes(y):
    return np.clip(np.asarray(y, np.float64), -448.0, 448.0).astype(np.float32).astype(ml_dtypes.float8_e4m3fn).view(np.uint8)


def e4m3fn_values(b):
    return np.asarray(b, np.uint8).view(ml_dtypes.float8_e4m3fn).astype(np.float64)


def setup_inputs():
    d = draw0()
    x0 = np.asarray(d['x']).astype(np.float64)
    s = (np.max(np.abs(x0), axis=(0,), keepdims=True) / 448.0).astype(np.float32)
    out = {}
    for k, v in d.items():
        if k == 'x':
            out['x_bytes'] = e4m3fn_bytes(x0 / s.astype(np.float64))
            out['x_scale'] = s
        else:
            out[k] = v
    return out


def reference(x_bytes, x_scale, t, lblk, rblk, kern, b, gain):
    return core(e4m3fn_values(x_bytes) * x_scale.astype(np.float64), t, lblk, rblk, kern, b, gain)

@@ -1,0 +1,248 @@
+from contextlib import ExitStack
+
+import concourse.mybir as mybir
+from concourse.masks import make_identity
+
+N, G, S = 1024, 4, 512
+D = G * S
+FLOPS = 2 * 2 * N * G * S * S
+
+F32 = mybir.dt.float32
+BF16 = mybir.dt.bfloat16
+U32 = mybir.dt.uint32
+U8 = mybir.dt.uint8
+FP8 = mybir.dt.float8_e4m3fn
+FP8X4 = mybir.dt.float8_e4m3fn_x4
+ACT = mybir.ActivationFunctionType
+ALU = mybir.AluOpType
+
+P = 128
+PACK = 4
+CHUNK = 512
+TILES = CHUNK // P
+CHUNKS = N // CHUNK
+UNITS = CHUNKS * G
+
+
+def tile_monarchgatedmixer_kernel(tc, x_bytes, x_scale, t, lblk, rblk, kern, b, gain, out):
+    nc = tc.nc
+    with ExitStack() as ctx:
+        keep = ctx.enter_context(tc.tile_pool(name="keep", bufs=1))
+        work = ctx.enter_context(tc.tile_pool(name="work", bufs=2))
+        psum = ctx.enter_context(tc.psum_pool(name="psum", bufs=8))
+        ctx.enter_context(tc.manual_schedule())
+
+        ident32 = keep.tile([P, P], F32, name="ident32")
+        make_identity(nc, ident32[:])
+        ident16 = keep.tile([P, P], BF16, name="ident16")
+        make_identity(nc, ident16[:])
+
+        scale_col = keep.tile([P, G, PACK], F32, name="scale_col")
+        nc.sync.dma_start(out=scale_col[:], in_=x_scale.rearrange("o (g p t) -> p (o g) t", p=P, t=PACK))
+        xbytes = []
+        w_raw = {}
+
+        def load_x(i):
+            xb = keep.tile([P, D], U8, name="xbytes%d" % i)
+            nc.sync.dma_start(out=xb[:], in_=x_bytes[i * P:(i + 1) * P, :])
+            xbytes.append(xb)
+
+        def load_w(side, src, g):
+            raw = keep.tile([P, PACK, S], BF16, name="raw_%s%d" % (side, g))
+            nc.sync.dma_start(out=raw[:], in_=src[g].rearrange("(p t) j -> p t j", t=PACK))
+            w_raw[(side, g)] = raw
+
+        for g in range(G):
+            load_x(g)
+            load_w("l", lblk, g)
+        chan16 = keep.tile([P, 3, G, PACK], BF16, name="chan16")
+        for i, src in enumerate((kern, b, gain)):
+            nc.sync.dma_start(out=chan16[:, i], in_=src.rearrange("h (p t) -> p h t", t=PACK))
+        load_x(4)
+        load_w("r", rblk, 0)
+        load_x(5)
+        gate = []
+
+        def load_t(c):
+            tt = keep.tile([P, TILES, D], BF16, name="gate%d" % c)
+            nc.sync.dma_start(out=tt[:], in_=t[c * CHUNK:(c + 1) * CHUNK, :].rearrange("(a p) d -> p a d", p=P))
+            gate.append(tt)
+
+        load_x(6)
+        load_w("r", rblk, 1)
+        load_t(0)
+        load_x(7)
+        load_w("r", rblk, 2)
+        load_w("r", rblk, 3)
+        load_t(1)
+
+        scale_row = keep.tile([P, D], F32, name="scale_row")
+        affine = keep.tile([P, 2, G * PACK], F32, name="affine")
+        half_gain = keep.tile([P, G, PACK], F32, name="half_gain")
+
+        xs, xt, xq, wi, wq, ge, mb, mq, th, acc2 = {}, {}, {}, {}, {}, {}, {}, {}, {}, {}
+
+        def quantize(src, name, pool, tag):
+            codes = pool.tile([P, S], U32, name=name + "_codes", tag=tag + "_codes", align_bytes=64, bufs=(1 if pool is keep else 3))
+            scales = pool.tile([P, S], U8, name=name + "_scales", tag=tag + "_scales", align_bytes=64, bufs=(1 if pool is keep else 3))
+            nc.vector.quantize_mx(out=codes[:].bitcast(FP8X4), scales=scales[:], in_=src)
+            return codes, scales
+
+        def spread_scale(g):
+            bank = psum.tile([P, PACK, P], F32, name="bank_sc", tag="bank")
+            for c in range(PACK):
+                nc.tensor.transpose(bank[:, c, :], scale_col[:, g, c:c + 1].to_broadcast([P, P]), ident32[:])
+            nc.scalar.copy(out=scale_row[:, g * S:(g + 1) * S].rearrange("p (n c) -> p n c", c=PACK),
+                           in_=bank[:].rearrange("p c n -> p n c"))
+
+        def scale_x(i, lo, hi):
+            if lo == 0:
+                xs[i] = work.tile([P, D], BF16, name="x_scaled", tag="x_scaled", bufs=2)
+            nc.vector.tensor_tensor(out=xs[i][:, lo:hi], in0=xbytes[i][:, lo:hi].bitcast(FP8), in1=scale_row[:, lo:hi], op=ALU.mult)
+
+        def turn_x(i):
+            c, a = divmod(i, TILES)
+            if a == 0:
+                xt[c] = work.tile([P, G, CHUNK * PACK], BF16, name="x_turned", tag="x_turned", bufs=1, align_bytes=64)
+            words = xs[i][:].bitcast(F32)
+            dst = xt[c][:].bitcast(F32).rearrange("p g (n u) -> p g n u", u=2)
+            for g0 in (0, 2):
+                bank = psum.tile([P, 2, 2, P], F32, name="bank_x", tag="bank")
+                for gg in range(2):
+                    for u in range(2):
+                        w0 = 256 * (g0 + gg)
+                        nc.tensor.transpose(bank[:, gg, u, :], words[:, w0 + u:w0 + 256:2], ident32[:])
+                nc.scalar.copy(out=dst[:, g0:g0 + 2, a * P:(a + 1) * P, :], in_=bank[:].rearrange("p g u n -> p g n u"))
+
+        def quant_x(c, g):
+            xq[(c, g)] = quantize(xt[c][:, g, :], "xq%d%d" % (c, g), keep, "xq%d%d" % (c, g))
+
+        def weave_direct(side, g):
+            wi[(side, g)] = work.tile([P, S * PACK], BF16, name="w_woven", tag="w_woven", bufs=3, align_bytes=64)
+            nc.scalar.copy(out=wi[(side, g)][:].rearrange("p (c i t) -> p c t i", i=4, t=PACK),
+                           in_=w_raw[(side, g)][:].rearrange("p t (c i) -> p c t i", i=4))
+
+        def weave_pe(side, g):
+            wi[(side, g)] = work.tile([P, S * PACK], BF16, name="w_woven", tag="w_woven", bufs=3, align_bytes=64)
+            for half in range(2):
+                bank = psum.tile([P, 2, P, PACK], BF16, name="bank_w", tag="bank")
+                for q in range(2):
+                    j0 = (2 * half + q) * P
+                    nc.tensor.matmul(bank[:, q], lhsT=ident16[:], rhs=w_raw[(side, g)][:, :, j0:j0 + P].rearrange("p t j -> p j t"),
+                                     start=True, stop=True)
+                nc.scalar.copy(out=wi[(side, g)][:, 1024 * half:1024 * (half + 1)], in_=bank[:].rearrange("p q j t -> p (q j t)"))
+
+        def quant_w(side, g):
+            wq[(side, g)] = quantize(wi[(side, g)][:], "wq%s%d" % (side, g), keep, "wq%s%d" % (side, g))
+
+        def left(u):
+            c, h = divmod(u, G)
+            ge[u] = work.tile([P, PACK, CHUNK], F32, name="gelu_out", tag="gelu_out", bufs=3)
+            for g in range(G):
+                bank = psum.tile([P, CHUNK], F32, name="bank_u", tag="bank")
+                lc, ls = wq[("l", g)]
+                xc, xsc = xq[(c, g)]
+                nc.tensor.matmul_mx(out=bank[:], lhsT=lc[:, h * P:(h + 1) * P].bitcast(FP8X4), lhsT_scale=ls[:, h * P:(h + 1) * P],
+                                    rhs=xc[:].bitcast(FP8X4), rhs_scale=xsc[:], start=True, stop=True)
+                col = h * PACK + g
+                nc.scalar.activation(out=ge[u][:, g, :], in_=bank[:], func=ACT.Gelu_apprx_tanh,
+                                     scale=affine[:, 0, col:col + 1], bias=affine[:, 1, col:col + 1])
+
+        def gain_m(u):
+            h = u % G
+            mb[u] = work.tile([P, CHUNK * PACK], BF16, name="m_woven", tag="m_woven", bufs=2, align_bytes=64)
+            nc.vector.tensor_tensor(
+                out=mb[u][:].rearrange("p (c i t) -> p c t i", i=2, t=PACK),
+                in0=ge[u][:].rearrange("p t (c i) -> p c t i", i=2),
+                in1=half_gain[:, h, :].unsqueeze(1).unsqueeze(3).to_broadcast([P, CHUNK // 2, PACK, 2]),
+                op=ALU.mult)
+
+        def quant_m(u):
+            mq[u] = quantize(mb[u][:], "mq", work, "mq")
+
+        def gate_tanh(u, half):
+            c, h = divmod(u, G)
+            th[(u, half)] = work.tile([P, 2 * G, P], F32, name="gate_tanh", tag="gate_tanh", bufs=4)
+            src = gate[c][:, 2 * half:2 * half + 2, :].rearrange("p a (g h i) -> p (a g) h i", g=G, h=G)
+            nc.scalar.activation(out=th[(u, half)][:], in_=src[:, :, h, :], func=ACT.Tanh, scale=0.5)
+
+        def right(u, a):
+            h = u % G
+            bank = psum.tile([P, S], F32, name="bank_v", tag="bank")
+            mc, ms = mq[u]
+            rc, rs = wq[("r", h)]
+            nc.tensor.matmul_mx(out=bank[:], lhsT=mc[:, a * P:(a + 1) * P].bitcast(FP8X4), lhsT_scale=ms[:, a * P:(a + 1) * P],
+                                rhs=rc[:].bitcast(FP8X4), rhs_scale=rs[:], start=True, stop=True)
+            acc2[(u, a)] = bank
+
+        def finish(u, a):
+            c, h = divmod(u, G)
+            res = work.tile([P, G, P], F32, name="res", tag="res", bufs=6)
+            half, aa = divmod(a, 2)
+            nc.vector.scalar_tensor_tensor(out=res[:], in0=th[(u, half)][:, aa * G:(aa + 1) * G, :], scalar=1.0,
+                                           in1=acc2[(u, a)][:].rearrange("p (i g) -> p g i", g=G),
+                                           op0=ALU.add, op1=ALU.mult)
+            r0 = c * CHUNK + a * P
+            dst = out[r0:r0 + P, :].rearrange("p (g h i) -> p g h i", g=G, h=G)
+            nc.sync.dma_start(out=dst[:, :, h, :], in_=res[:])
+
+        for g in range(G):
+            spread_scale(g)
+            scale_x(0, g * S, (g + 1) * S)
+        weave_direct("l", 0)
+        turn_x(0)
+        scale_x(1, 0, D)
+        quant_w("l", 0)
+        weave_direct("l", 1)
+        turn_x(1)
+        scale_x(2, 0, D)
+        quant_w("l", 1)
+        weave_pe("l", 2)
+        turn_x(2)
+        scale_x(3, 0, D)
+        quant_w("l", 2)
+        weave_pe("l", 3)
+        turn_x(3)
+        nc.vector.tensor_copy(out=affine[:], in_=chan16[:, 0:2].rearrange("p i h t -> p i (h t)"))
+        nc.vector.tensor_scalar(out=half_gain[:], in0=chan16[:, 2], scalar1=0.5, scalar2=None, op0=ALU.mult)
+        scale_x(4, 0, D)
+        quant_w("l", 3)
+        for g in range(G):
+            quant_x(0, g)
+
+        left(0)
+        turn_x(4)
+        weave_pe("r", 0)
+        scale_x(5, 0, D)
+        left(1)
+        turn_x(5)
+        gain_m(0)
+        quant_w("r", 0)
+        quant_m(0)
+        for u in range(UNITS):
+            gate_tanh(u, 0)
+            gate_tanh(u, 1)
+            if u + 1 < G:
+                weave_pe("r", u + 1)
+            if u < 2:
+                scale_x(6 + u, 0, D)
+                turn_x(6 + u)
+            if u == 2:
+                for g in range(G):
+                    quant_x(1, g)
+            right(u, 0)
+            right(u, 1)
+            if u + 2 < UNITS:
+                left(u + 2)
+            right(u, 2)
+            right(u, 3)
+            if u + 1 < UNITS:
+                gain_m(u + 1)
+            finish(u, 0)
+            finish(u, 1)
+            if u + 1 < G:
+                quant_w("r", u + 1)
+            if u + 1 < UNITS:
+                quant_m(u + 1)
+            finish(u, 2)
+            finish(u, 3)

@@ -22,6 +22,7 @@ CHUNK = 512
 TILES = CHUNK // P
 CHUNKS = N // CHUNK
 UNITS = CHUNKS * G
+POOL_TOKENS = (512, 384, 256)
 
 
 def tile_monarchgatedmixer_kernel(tc, x_bytes, x_scale, t, lblk, rblk, kern, b, gain, out):
@@ -29,9 +30,13 @@ def tile_monarchgatedmixer_kernel(tc, x_bytes, x_scale, t, lblk, rblk, kern, b, 
     with ExitStack() as ctx:
         keep = ctx.enter_context(tc.tile_pool(name="keep", bufs=1))
         work = ctx.enter_context(tc.tile_pool(name="work", bufs=2))
-        psum = ctx.enter_context(tc.psum_pool(name="psum", bufs=8))
+        psum = ctx.enter_context(tc.psum_pool(name="psum", bufs=4))
         ctx.enter_context(tc.manual_schedule())
 
+        zero_in = keep.tile([P, 1], F32, name="zero_in")
+        zero_bias = keep.tile([P, 1], F32, name="zero_bias")
+        nc.vector.memset(zero_in[:], 0.0)
+        nc.scalar.activation(out=zero_bias[:], in_=zero_in[:], func=ACT.Gelu_apprx_tanh)
         ident32 = keep.tile([P, P], F32, name="ident32")
         make_identity(nc, ident32[:])
         ident16 = keep.tile([P, P], BF16, name="ident16")
@@ -58,28 +63,32 @@ def tile_monarchgatedmixer_kernel(tc, x_bytes, x_scale, t, lblk, rblk, kern, b, 
         chan16 = keep.tile([P, 3, G, PACK], BF16, name="chan16")
         for i, src in enumerate((kern, b, gain)):
             nc.sync.dma_start(out=chan16[:, i], in_=src.rearrange("h (p t) -> p h t", t=PACK))
+        gate = {}
+
+        def load_t(c, half):
+            tt = keep.tile([P, 2, D], BF16, name="gate%d%d" % (c, half))
+            r0 = c * CHUNK + half * 2 * P
+            nc.sync.dma_start(out=tt[:], in_=t[r0:r0 + 2 * P, :].rearrange("(a p) d -> p a d", p=P))
+            gate[(c, half)] = tt
+
         load_x(4)
-        load_w("r", rblk, 0)
+        load_t(0, 0)
         load_x(5)
-        gate = []
-
-        def load_t(c):
-            tt = keep.tile([P, TILES, D], BF16, name="gate%d" % c)
-            nc.sync.dma_start(out=tt[:], in_=t[c * CHUNK:(c + 1) * CHUNK, :].rearrange("(a p) d -> p a d", p=P))
-            gate.append(tt)
-
         load_x(6)
-        load_w("r", rblk, 1)
-        load_t(0)
+        load_w("r", rblk, 0)
         load_x(7)
+        load_t(0, 1)
+        load_w("r", rblk, 1)
         load_w("r", rblk, 2)
+        load_t(1, 0)
         load_w("r", rblk, 3)
-        load_t(1)
+        load_t(1, 1)
 
-        scale_row = keep.tile([P, D], F32, name="scale_row")
         affine = keep.tile([P, 2, G * PACK], F32, name="affine")
-        half_gain = keep.tile([P, G, PACK], F32, name="half_gain")
+        half_gain = keep.tile([P, G, PACK], BF16, name="half_gain")
+        gain_bank = psum.tile([P, G, PACK], F32, name="gain_bank", tag="gain_bank", bufs=1)
 
+        xbank = {}
         xs, xt, xq, wi, wq, ge, mb, mq, th, acc2 = {}, {}, {}, {}, {}, {}, {}, {}, {}, {}
 
         def quantize(src, name, pool, tag):
@@ -88,87 +97,99 @@ def tile_monarchgatedmixer_kernel(tc, x_bytes, x_scale, t, lblk, rblk, kern, b, 
             nc.vector.quantize_mx(out=codes[:].bitcast(FP8X4), scales=scales[:], in_=src)
             return codes, scales
 
-        def spread_scale(g):
-            bank = psum.tile([P, PACK, P], F32, name="bank_sc", tag="bank")
-            for c in range(PACK):
-                nc.tensor.transpose(bank[:, c, :], scale_col[:, g, c:c + 1].to_broadcast([P, P]), ident32[:])
-            nc.scalar.copy(out=scale_row[:, g * S:(g + 1) * S].rearrange("p (n c) -> p n c", c=PACK),
-                           in_=bank[:].rearrange("p c n -> p n c"))
-
-        def scale_x(i, lo, hi):
+        def widen_x(i, lo, hi):
             if lo == 0:
-                xs[i] = work.tile([P, D], BF16, name="x_scaled", tag="x_scaled", bufs=2)
-            nc.vector.tensor_tensor(out=xs[i][:, lo:hi], in0=xbytes[i][:, lo:hi].bitcast(FP8), in1=scale_row[:, lo:hi], op=ALU.mult)
+                xs[i] = work.tile([P, D], BF16, name="x_wide", tag="x_wide", bufs=3)
+            nc.scalar.copy(out=xs[i][:, lo:hi], in_=xbytes[i][:, lo:hi].bitcast(FP8))
 
         def turn_x(i):
-            c, a = divmod(i, TILES)
-            if a == 0:
-                xt[c] = work.tile([P, G, CHUNK * PACK], BF16, name="x_turned", tag="x_turned", bufs=1, align_bytes=64)
             words = xs[i][:].bitcast(F32)
-            dst = xt[c][:].bitcast(F32).rearrange("p g (n u) -> p g n u", u=2)
             for g0 in (0, 2):
-                bank = psum.tile([P, 2, 2, P], F32, name="bank_x", tag="bank")
+                bank = psum.tile([P, 2, 2, P], F32, name="bank_x", tag="to_vector", bufs=4)
                 for gg in range(2):
                     for u in range(2):
                         w0 = 256 * (g0 + gg)
-                        nc.tensor.transpose(bank[:, gg, u, :], words[:, w0 + u:w0 + 256:2], ident32[:])
-                nc.scalar.copy(out=dst[:, g0:g0 + 2, a * P:(a + 1) * P, :], in_=bank[:].rearrange("p g u n -> p g n u"))
+                        nc.tensor.transpose(bank[:, u, gg, :], words[:, w0 + u:w0 + 256:2], ident32[:])
+                xbank[(i, g0)] = bank
+
+        def scale_x(i):
+            c, a = divmod(i, TILES)
+            if a == 0:
+                xt[c] = work.tile([P, G, CHUNK, 2, 2], BF16, name="x_turned", tag="x_turned", bufs=1, align_bytes=64)
+            for g0 in (0, 2):
+                halves = xbank[(i, g0)][:].rearrange("p u g n -> p (u g n)").bitcast(BF16)
+                nc.vector.tensor_tensor(
+                    out=xt[c][:, g0:g0 + 2, a * P:(a + 1) * P],
+                    in0=halves.rearrange("p (u g n e) -> p g n u e", u=2, g=2, e=2),
+                    in1=scale_col[:, g0:g0 + 2, :].rearrange("p g (u e) -> p g u e", u=2).unsqueeze(2).to_broadcast([P, 2, P, 2, 2]),
+                    op=ALU.mult)
 
         def quant_x(c, g):
-            xq[(c, g)] = quantize(xt[c][:, g, :], "xq%d%d" % (c, g), keep, "xq%d%d" % (c, g))
+            xq[(c, g)] = quantize(xt[c][:, g].rearrange("p n u e -> p (n u e)"), "xq%d%d" % (c, g), keep, "xq%d%d" % (c, g))
 
-        def weave_direct(side, g):
-            wi[(side, g)] = work.tile([P, S * PACK], BF16, name="w_woven", tag="w_woven", bufs=3, align_bytes=64)
-            nc.scalar.copy(out=wi[(side, g)][:].rearrange("p (c i t) -> p c t i", i=4, t=PACK),
-                           in_=w_raw[(side, g)][:].rearrange("p t (c i) -> p c t i", i=4))
+        def weave_pool(side, g):
+            wi[(side, g)] = work.tile([P, S * PACK], BF16, name="w_woven", tag="w_woven", bufs=4, align_bytes=64)
+            nc.gpsimd.tensor_scalar(out=wi[(side, g)][:].rearrange("p (j t) -> p j t", t=PACK),
+                                    in0=w_raw[(side, g)][:].rearrange("p t j -> p j t"),
+                                    scalar1=1.0, scalar2=0.0, op0=ALU.mult, op1=ALU.add)
 
-        def weave_pe(side, g):
-            wi[(side, g)] = work.tile([P, S * PACK], BF16, name="w_woven", tag="w_woven", bufs=3, align_bytes=64)
-            for half in range(2):
-                bank = psum.tile([P, 2, P, PACK], BF16, name="bank_w", tag="bank")
-                for q in range(2):
-                    j0 = (2 * half + q) * P
-                    nc.tensor.matmul(bank[:, q], lhsT=ident16[:], rhs=w_raw[(side, g)][:, :, j0:j0 + P].rearrange("p t j -> p j t"),
-                                     start=True, stop=True)
-                nc.scalar.copy(out=wi[(side, g)][:, 1024 * half:1024 * (half + 1)], in_=bank[:].rearrange("p q j t -> p (q j t)"))
+        def weave_pe(side, g, half):
+            if half == 0:
+                wi[(side, g)] = work.tile([P, S * PACK], BF16, name="w_woven", tag="w_woven", bufs=4, align_bytes=64)
+            bank = psum.tile([P, 2, P, PACK], BF16, name="bank_w", tag="to_scalar", bufs=3)
+            for q in range(2):
+                j0 = (2 * half + q) * P
+                nc.tensor.matmul(bank[:, q], lhsT=ident16[:], rhs=w_raw[(side, g)][:, :, j0:j0 + P].rearrange("p t j -> p j t"),
+                                 start=True, stop=True)
+            nc.scalar.copy(out=wi[(side, g)][:, 1024 * half:1024 * (half + 1)], in_=bank[:].rearrange("p q j t -> p (q j t)"))
 
         def quant_w(side, g):
             wq[(side, g)] = quantize(wi[(side, g)][:], "wq%s%d" % (side, g), keep, "wq%s%d" % (side, g))
 
-        def left(u):
+        def left(u, g):
             c, h = divmod(u, G)
-            ge[u] = work.tile([P, PACK, CHUNK], F32, name="gelu_out", tag="gelu_out", bufs=3)
-            for g in range(G):
-                bank = psum.tile([P, CHUNK], F32, name="bank_u", tag="bank")
-                lc, ls = wq[("l", g)]
-                xc, xsc = xq[(c, g)]
-                nc.tensor.matmul_mx(out=bank[:], lhsT=lc[:, h * P:(h + 1) * P].bitcast(FP8X4), lhsT_scale=ls[:, h * P:(h + 1) * P],
-                                    rhs=xc[:].bitcast(FP8X4), rhs_scale=xsc[:], start=True, stop=True)
-                col = h * PACK + g
-                nc.scalar.activation(out=ge[u][:, g, :], in_=bank[:], func=ACT.Gelu_apprx_tanh,
-                                     scale=affine[:, 0, col:col + 1], bias=affine[:, 1, col:col + 1])
+            if g == 0:
+                ge[u] = work.tile([P, PACK, CHUNK], F32, name="gelu_out", tag="gelu_out", bufs=3)
+            bank = psum.tile([P, CHUNK], F32, name="bank_u", tag="to_scalar", bufs=3)
+            lc, ls = wq[("l", g)]
+            xc, xsc = xq[(c, g)]
+            nc.tensor.matmul_mx(out=bank[:], lhsT=lc[:, h * P:(h + 1) * P].bitcast(FP8X4), lhsT_scale=ls[:, h * P:(h + 1) * P],
+                                rhs=xc[:].bitcast(FP8X4), rhs_scale=xsc[:], start=True, stop=True)
+            col = h * PACK + g
+            nc.scalar.activation(out=ge[u][:, g, :], in_=bank[:], func=ACT.Gelu_apprx_tanh,
+                                 scale=affine[:, 0, col:col + 1], bias=affine[:, 1, col:col + 1])
 
-        def gain_m(u):
+        def gain_pool(u):
             h = u % G
-            mb[u] = work.tile([P, CHUNK * PACK], BF16, name="m_woven", tag="m_woven", bufs=2, align_bytes=64)
+            split = POOL_TOKENS[min(u, 2)]
+            mb[u] = work.tile([P, CHUNK, PACK], BF16, name="m_woven", tag="m_woven", bufs=1, align_bytes=64)
+            nc.gpsimd.tensor_tensor(
+                out=mb[u][:, :split, :],
+                in0=ge[u][:, :, :split].rearrange("p t n -> p n t"),
+                in1=half_gain[:, h, :].unsqueeze(1).to_broadcast([P, split, PACK]),
+                op=ALU.mult)
+
+        def gain_vector(u):
+            h = u % G
+            split = POOL_TOKENS[min(u, 2)]
             nc.vector.tensor_tensor(
-                out=mb[u][:].rearrange("p (c i t) -> p c t i", i=2, t=PACK),
-                in0=ge[u][:].rearrange("p t (c i) -> p c t i", i=2),
-                in1=half_gain[:, h, :].unsqueeze(1).unsqueeze(3).to_broadcast([P, CHUNK // 2, PACK, 2]),
+                out=mb[u][:, split:, :].rearrange("p (c i) t -> p c t i", i=2),
+                in0=ge[u][:, :, split:].rearrange("p t (c i) -> p c t i", i=2),
+                in1=gain_bank[:, h, :].unsqueeze(1).unsqueeze(3).to_broadcast([P, (CHUNK - split) // 2, PACK, 2]),
                 op=ALU.mult)
 
         def quant_m(u):
-            mq[u] = quantize(mb[u][:], "mq", work, "mq")
+            mq[u] = quantize(mb[u][:].rearrange("p n t -> p (n t)"), "mq", work, "mq")
 
         def gate_tanh(u, half):
             c, h = divmod(u, G)
-            th[(u, half)] = work.tile([P, 2 * G, P], F32, name="gate_tanh", tag="gate_tanh", bufs=4)
-            src = gate[c][:, 2 * half:2 * half + 2, :].rearrange("p a (g h i) -> p (a g) h i", g=G, h=G)
-            nc.scalar.activation(out=th[(u, half)][:], in_=src[:, :, h, :], func=ACT.Tanh, scale=0.5)
+            th[(u, half)] = work.tile([P, 2 * G, P], F32, name="gate_tanh", tag="gate_tanh%d" % half, bufs=3 - half)
+            src = gate[(c, half)][:].rearrange("p a (g h i) -> p (a g) h i", g=G, h=G)
+            nc.scalar.activation(out=th[(u, half)][:], in_=src[:, :, h, :], func=ACT.Tanh, scale=0.5, bias=zero_bias[:])
 
         def right(u, a):
             h = u % G
-            bank = psum.tile([P, S], F32, name="bank_v", tag="bank")
+            bank = psum.tile([P, S], F32, name="bank_v", tag="to_vector", bufs=4)
             mc, ms = mq[u]
             rc, rs = wq[("r", h)]
             nc.tensor.matmul_mx(out=bank[:], lhsT=mc[:, a * P:(a + 1) * P].bitcast(FP8X4), lhsT_scale=ms[:, a * P:(a + 1) * P],
@@ -186,60 +207,74 @@ def tile_monarchgatedmixer_kernel(tc, x_bytes, x_scale, t, lblk, rblk, kern, b, 
             dst = out[r0:r0 + P, :].rearrange("p (g h i) -> p g h i", g=G, h=G)
             nc.sync.dma_start(out=dst[:, :, h, :], in_=res[:])
 
-        for g in range(G):
-            spread_scale(g)
-            scale_x(0, g * S, (g + 1) * S)
-        weave_direct("l", 0)
+        widen_x(0, 0, D // 2)
+        widen_x(0, D // 2, D)
         turn_x(0)
-        scale_x(1, 0, D)
-        quant_w("l", 0)
-        weave_direct("l", 1)
-        turn_x(1)
-        scale_x(2, 0, D)
-        quant_w("l", 1)
-        weave_pe("l", 2)
-        turn_x(2)
-        scale_x(3, 0, D)
-        quant_w("l", 2)
-        weave_pe("l", 3)
-        turn_x(3)
-        nc.vector.tensor_copy(out=affine[:], in_=chan16[:, 0:2].rearrange("p i h t -> p i (h t)"))
-        nc.vector.tensor_scalar(out=half_gain[:], in0=chan16[:, 2], scalar1=0.5, scalar2=None, op0=ALU.mult)
-        scale_x(4, 0, D)
-        quant_w("l", 3)
+        for i in range(1, TILES + 1):
+            if i < TILES:
+                weave_pool("l", i - 1)
+            widen_x(i, 0, D)
+            if i == TILES:
+                weave_pe("l", 3, 0)
+                weave_pe("l", 3, 1)
+            turn_x(i)
+            scale_x(i - 1)
+        widen_x(5, 0, D)
+        widen_x(6, 0, D)
+        gate_tanh(0, 0)
         for g in range(G):
+            quant_w("l", g)
+            if g == 0:
+                nc.vector.tensor_copy(out=affine[:], in_=chan16[:, 0:2].rearrange("p i h t -> p i (h t)"))
+                nc.vector.tensor_scalar(out=half_gain[:], in0=chan16[:, 2], scalar1=0.5, scalar2=None, op0=ALU.mult)
             quant_x(0, g)
-
-        left(0)
-        turn_x(4)
-        weave_pe("r", 0)
-        scale_x(5, 0, D)
-        left(1)
+            left(0, g)
+            if g < 2:
+                weave_pe("r", 0, g)
+        gain_pool(0)
         turn_x(5)
-        gain_m(0)
+        scale_x(4)
+        for g in range(G):
+            left(1, g)
+        nc.tensor.matmul(gain_bank[:], lhsT=ident16[:], rhs=half_gain[:], start=True, stop=True)
+        widen_x(7, 0, D)
+        turn_x(6)
+        scale_x(5)
+        gate_tanh(0, 1)
+        turn_x(7)
+        scale_x(6)
+        gate_tanh(1, 0)
+        weave_pe("r", 1, 0)
+        weave_pe("r", 1, 1)
         quant_w("r", 0)
         quant_m(0)
+        scale_x(7)
         for u in range(UNITS):
-            gate_tanh(u, 0)
-            gate_tanh(u, 1)
-            if u + 1 < G:
-                weave_pe("r", u + 1)
-            if u < 2:
-                scale_x(6 + u, 0, D)
-                turn_x(6 + u)
-            if u == 2:
-                for g in range(G):
-                    quant_x(1, g)
+            if u + 1 < UNITS:
+                gain_pool(u + 1)
+            if u + 2 < UNITS:
+                for g in range(G - 1):
+                    left(u + 2, g)
             right(u, 0)
             right(u, 1)
             if u + 2 < UNITS:
-                left(u + 2)
+                left(u + 2, G - 1)
+            if u + 1 < UNITS:
+                gate_tanh(u + 1, 1)
+            if u + 2 < UNITS:
+                gate_tanh(u + 2, 0)
+            if u + 2 < G:
+                weave_pe("r", u + 2, 0)
+                weave_pe("r", u + 2, 1)
             right(u, 2)
             right(u, 3)
             if u + 1 < UNITS:
-                gain_m(u + 1)
+                gain_vector(u + 1)
             finish(u, 0)
             finish(u, 1)
+            if u == 0:
+                for g in range(G):
+                    quant_x(1, g)
             if u + 1 < G:
                 quant_w("r", u + 1)
             if u + 1 < UNITS:

@@ -20,9 +20,12 @@ P = 128
 PACK = 4
 CHUNK = 512
 TILES = CHUNK // P
-CHUNKS = N // CHUNK
-UNITS = CHUNKS * G
-POOL_TOKENS = (512, 384, 256)
+UNITS = (N // CHUNK) * G
+GROUP_WORDS = S // 2
+
+POOL_TOKENS_UNIT0, POOL_TOKENS_UNIT1, POOL_TOKENS_LATER = 512, 384, 256
+
+VECTOR_BANKS, SCALAR_BANKS = 4, 3
 
 
 def tile_monarchgatedmixer_kernel(tc, x_bytes, x_scale, t, lblk, rblk, kern, b, gain, out):
@@ -30,7 +33,7 @@ def tile_monarchgatedmixer_kernel(tc, x_bytes, x_scale, t, lblk, rblk, kern, b, 
     with ExitStack() as ctx:
         keep = ctx.enter_context(tc.tile_pool(name="keep", bufs=1))
         work = ctx.enter_context(tc.tile_pool(name="work", bufs=2))
-        psum = ctx.enter_context(tc.psum_pool(name="psum", bufs=4))
+        psum = ctx.enter_context(tc.psum_pool(name="psum", bufs=1))
         ctx.enter_context(tc.manual_schedule())
 
         zero_in = keep.tile([P, 1], F32, name="zero_in")
@@ -42,39 +45,35 @@ def tile_monarchgatedmixer_kernel(tc, x_bytes, x_scale, t, lblk, rblk, kern, b, 
         ident16 = keep.tile([P, P], BF16, name="ident16")
         make_identity(nc, ident16[:])
 
-        scale_col = keep.tile([P, G, PACK], F32, name="scale_col")
-        nc.sync.dma_start(out=scale_col[:], in_=x_scale.rearrange("o (g p t) -> p (o g) t", p=P, t=PACK))
-        xbytes = []
-        w_raw = {}
+        xbytes, w_raw, gate_in = {}, {}, {}
 
-        def load_x(i):
-            xb = keep.tile([P, D], U8, name="xbytes%d" % i)
-            nc.sync.dma_start(out=xb[:], in_=x_bytes[i * P:(i + 1) * P, :])
-            xbytes.append(xb)
+        def load_x(tile):
+            xbytes[tile] = keep.tile([P, D], U8, name="xbytes%d" % tile)
+            nc.sync.dma_start(out=xbytes[tile][:], in_=x_bytes[tile * P:(tile + 1) * P, :])
 
         def load_w(side, src, g):
-            raw = keep.tile([P, PACK, S], BF16, name="raw_%s%d" % (side, g))
-            nc.sync.dma_start(out=raw[:], in_=src[g].rearrange("(p t) j -> p t j", t=PACK))
-            w_raw[(side, g)] = raw
+            w_raw[(side, g)] = keep.tile([P, PACK, S], BF16, name="raw_%s%d" % (side, g))
+            nc.sync.dma_start(out=w_raw[(side, g)][:], in_=src[g].rearrange("(p t) j -> p t j", t=PACK))
 
-        for g in range(G):
-            load_x(g)
-            load_w("l", lblk, g)
+        def load_t(chunk, pair):
+            gate_in[(chunk, pair)] = keep.tile([P, 2, D], BF16, name="gate_in%d%d" % (chunk, pair))
+            row = chunk * CHUNK + pair * 2 * P
+            nc.sync.dma_start(out=gate_in[(chunk, pair)][:], in_=t[row:row + 2 * P, :].rearrange("(a p) d -> p a d", p=P))
+
+        scale_col = keep.tile([P, G, PACK], F32, name="scale_col")
         chan16 = keep.tile([P, 3, G, PACK], BF16, name="chan16")
+        load_x(0)
+        nc.sync.dma_start(out=scale_col[:], in_=x_scale.rearrange("o (g p t) -> p (o g) t", p=P, t=PACK))
+        for g in range(G - 1):
+            load_w("l", lblk, g)
+            load_x(g + 1)
+        load_x(4)
+        load_w("l", lblk, G - 1)
         for i, src in enumerate((kern, b, gain)):
             nc.sync.dma_start(out=chan16[:, i], in_=src.rearrange("h (p t) -> p h t", t=PACK))
-        gate = {}
-
-        def load_t(c, half):
-            tt = keep.tile([P, 2, D], BF16, name="gate%d%d" % (c, half))
-            r0 = c * CHUNK + half * 2 * P
-            nc.sync.dma_start(out=tt[:], in_=t[r0:r0 + 2 * P, :].rearrange("(a p) d -> p a d", p=P))
-            gate[(c, half)] = tt
-
-        load_x(4)
-        load_t(0, 0)
         load_x(5)
         load_x(6)
+        load_t(0, 0)
         load_w("r", rblk, 0)
         load_x(7)
         load_t(0, 1)
@@ -86,142 +85,152 @@ def tile_monarchgatedmixer_kernel(tc, x_bytes, x_scale, t, lblk, rblk, kern, b, 
 
         affine = keep.tile([P, 2, G * PACK], F32, name="affine")
         half_gain = keep.tile([P, G, PACK], BF16, name="half_gain")
-        gain_bank = psum.tile([P, G, PACK], F32, name="gain_bank", tag="gain_bank", bufs=1)
+        gain_bank = psum.tile([P, G, PACK], F32, name="gain_bank")
 
-        xbank = {}
-        xs, xt, xq, wi, wq, ge, mb, mq, th, acc2 = {}, {}, {}, {}, {}, {}, {}, {}, {}, {}
+        x_wide, x_banks, x_inter, x_mx = {}, {}, {}, {}
+        w_inter, w_mx = {}, {}
+        gelu_out, m_inter, m_mx, gate_tanh, v_banks = {}, {}, {}, {}, {}
 
-        def quantize(src, name, pool, tag):
-            codes = pool.tile([P, S], U32, name=name + "_codes", tag=tag + "_codes", align_bytes=64, bufs=(1 if pool is keep else 3))
-            scales = pool.tile([P, S], U8, name=name + "_scales", tag=tag + "_scales", align_bytes=64, bufs=(1 if pool is keep else 3))
+        def quantize(src, pool, name, bufs):
+            codes = pool.tile([P, S], U32, name=name + "_codes", align_bytes=64, bufs=bufs)
+            scales = pool.tile([P, S], U8, name=name + "_scales", align_bytes=64, bufs=bufs)
             nc.vector.quantize_mx(out=codes[:].bitcast(FP8X4), scales=scales[:], in_=src)
             return codes, scales
 
-        def widen_x(i, lo, hi):
+        def mx_product(bank, stationary, first_col, moving):
+            cols = slice(first_col, first_col + P)
+            nc.tensor.matmul_mx(out=bank[:], lhsT=stationary[0][:, cols].bitcast(FP8X4), lhsT_scale=stationary[1][:, cols],
+                                rhs=moving[0][:].bitcast(FP8X4), rhs_scale=moving[1][:], start=True, stop=True)
+
+        def widen_x(tile, lo=0, hi=D):
             if lo == 0:
-                xs[i] = work.tile([P, D], BF16, name="x_wide", tag="x_wide", bufs=3)
-            nc.scalar.copy(out=xs[i][:, lo:hi], in_=xbytes[i][:, lo:hi].bitcast(FP8))
+                x_wide[tile] = work.tile([P, D], BF16, name="x_wide", bufs=3)
+            nc.scalar.copy(out=x_wide[tile][:, lo:hi], in_=xbytes[tile][:, lo:hi].bitcast(FP8))
 
-        def turn_x(i):
-            words = xs[i][:].bitcast(F32)
+        def turn_x(tile):
+            words = x_wide[tile][:].bitcast(F32)
             for g0 in (0, 2):
-                bank = psum.tile([P, 2, 2, P], F32, name="bank_x", tag="to_vector", bufs=4)
-                for gg in range(2):
+                bank = psum.tile([P, 2, 2, P], F32, name="bank_x", tag="to_vector", bufs=VECTOR_BANKS)
+                for dg in range(2):
+                    w0 = GROUP_WORDS * (g0 + dg)
                     for u in range(2):
-                        w0 = 256 * (g0 + gg)
-                        nc.tensor.transpose(bank[:, u, gg, :], words[:, w0 + u:w0 + 256:2], ident32[:])
-                xbank[(i, g0)] = bank
+                        nc.tensor.transpose(bank[:, u, dg, :], words[:, w0 + u:w0 + GROUP_WORDS:2], ident32[:])
+                x_banks[(tile, g0)] = bank
 
-        def scale_x(i):
-            c, a = divmod(i, TILES)
+        def scale_x(tile):
+            chunk, a = divmod(tile, TILES)
             if a == 0:
-                xt[c] = work.tile([P, G, CHUNK, 2, 2], BF16, name="x_turned", tag="x_turned", bufs=1, align_bytes=64)
+                x_inter[chunk] = work.tile([P, G, CHUNK, 2, 2], BF16, name="x_inter", bufs=1, align_bytes=64)
             for g0 in (0, 2):
-                halves = xbank[(i, g0)][:].rearrange("p u g n -> p (u g n)").bitcast(BF16)
+                values = x_banks[(tile, g0)][:].rearrange("p u g n -> p (u g n)").bitcast(BF16)
+                scales = scale_col[:, g0:g0 + 2, :].rearrange("p g (u e) -> p g u e", u=2)
                 nc.vector.tensor_tensor(
-                    out=xt[c][:, g0:g0 + 2, a * P:(a + 1) * P],
-                    in0=halves.rearrange("p (u g n e) -> p g n u e", u=2, g=2, e=2),
-                    in1=scale_col[:, g0:g0 + 2, :].rearrange("p g (u e) -> p g u e", u=2).unsqueeze(2).to_broadcast([P, 2, P, 2, 2]),
+                    out=x_inter[chunk][:, g0:g0 + 2, a * P:(a + 1) * P],
+                    in0=values.rearrange("p (u g n e) -> p g n u e", u=2, g=2, e=2),
+                    in1=scales.unsqueeze(2).to_broadcast([P, 2, P, 2, 2]),
                     op=ALU.mult)
 
-        def quant_x(c, g):
-            xq[(c, g)] = quantize(xt[c][:, g].rearrange("p n u e -> p (n u e)"), "xq%d%d" % (c, g), keep, "xq%d%d" % (c, g))
+        def quant_x(chunk, g):
+            src = x_inter[chunk][:, g].rearrange("p n u e -> p (n u e)")
+            x_mx[(chunk, g)] = quantize(src, keep, "x_mx%d%d" % (chunk, g), 1)
 
-        def weave_pool(side, g):
-            wi[(side, g)] = work.tile([P, S * PACK], BF16, name="w_woven", tag="w_woven", bufs=4, align_bytes=64)
-            nc.gpsimd.tensor_scalar(out=wi[(side, g)][:].rearrange("p (j t) -> p j t", t=PACK),
+        def new_w_inter(side, g):
+            w_inter[(side, g)] = work.tile([P, S * PACK], BF16, name="w_inter", bufs=G, align_bytes=64)
+            return w_inter[(side, g)]
+
+        def interleave_on_pool(side, g):
+            nc.gpsimd.tensor_scalar(out=new_w_inter(side, g)[:].rearrange("p (j t) -> p j t", t=PACK),
                                     in0=w_raw[(side, g)][:].rearrange("p t j -> p j t"),
                                     scalar1=1.0, scalar2=0.0, op0=ALU.mult, op1=ALU.add)
 
-        def weave_pe(side, g, half):
-            if half == 0:
-                wi[(side, g)] = work.tile([P, S * PACK], BF16, name="w_woven", tag="w_woven", bufs=4, align_bytes=64)
-            bank = psum.tile([P, 2, P, PACK], BF16, name="bank_w", tag="to_scalar", bufs=3)
-            for q in range(2):
-                j0 = (2 * half + q) * P
-                nc.tensor.matmul(bank[:, q], lhsT=ident16[:], rhs=w_raw[(side, g)][:, :, j0:j0 + P].rearrange("p t j -> p j t"),
-                                 start=True, stop=True)
-            nc.scalar.copy(out=wi[(side, g)][:, 1024 * half:1024 * (half + 1)], in_=bank[:].rearrange("p q j t -> p (q j t)"))
+        def interleave_on_scalar(side, g):
+            nc.scalar.copy(out=new_w_inter(side, g)[:].rearrange("p (c i t) -> p c t i", i=4, t=PACK),
+                           in_=w_raw[(side, g)][:].rearrange("p t (c i) -> p c t i", i=4))
+
+        def interleave_on_tensor(side, g):
+            dst = new_w_inter(side, g)
+            for half in range(2):
+                bank = psum.tile([P, 2, P, PACK], BF16, name="bank_w", tag="to_scalar", bufs=SCALAR_BANKS)
+                for q in range(2):
+                    j0 = (2 * half + q) * P
+                    nc.tensor.matmul(bank[:, q], lhsT=ident16[:],
+                                     rhs=w_raw[(side, g)][:, :, j0:j0 + P].rearrange("p t j -> p j t"),
+                                     start=True, stop=True)
+                width = 2 * P * PACK
+                nc.scalar.copy(out=dst[:, width * half:width * (half + 1)], in_=bank[:].rearrange("p q j t -> p (q j t)"))
 
         def quant_w(side, g):
-            wq[(side, g)] = quantize(wi[(side, g)][:], "wq%s%d" % (side, g), keep, "wq%s%d" % (side, g))
+            w_mx[(side, g)] = quantize(w_inter[(side, g)][:], keep, "w_mx_%s%d" % (side, g), 1)
 
-        def left(u, g):
-            c, h = divmod(u, G)
+        def left(unit, g):
+            chunk, h = divmod(unit, G)
             if g == 0:
-                ge[u] = work.tile([P, PACK, CHUNK], F32, name="gelu_out", tag="gelu_out", bufs=3)
-            bank = psum.tile([P, CHUNK], F32, name="bank_u", tag="to_scalar", bufs=3)
-            lc, ls = wq[("l", g)]
-            xc, xsc = xq[(c, g)]
-            nc.tensor.matmul_mx(out=bank[:], lhsT=lc[:, h * P:(h + 1) * P].bitcast(FP8X4), lhsT_scale=ls[:, h * P:(h + 1) * P],
-                                rhs=xc[:].bitcast(FP8X4), rhs_scale=xsc[:], start=True, stop=True)
+                gelu_out[unit] = work.tile([P, PACK, CHUNK], F32, name="gelu_out", bufs=3)
+            bank = psum.tile([P, CHUNK], F32, name="bank_u", tag="to_scalar", bufs=SCALAR_BANKS)
+            mx_product(bank, w_mx[("l", g)], h * P, x_mx[(chunk, g)])
             col = h * PACK + g
-            nc.scalar.activation(out=ge[u][:, g, :], in_=bank[:], func=ACT.Gelu_apprx_tanh,
+            nc.scalar.activation(out=gelu_out[unit][:, g, :], in_=bank[:], func=ACT.Gelu_apprx_tanh,
                                  scale=affine[:, 0, col:col + 1], bias=affine[:, 1, col:col + 1])
 
-        def gain_pool(u):
-            h = u % G
-            split = POOL_TOKENS[min(u, 2)]
-            mb[u] = work.tile([P, CHUNK, PACK], BF16, name="m_woven", tag="m_woven", bufs=1, align_bytes=64)
+        def pool_tokens(unit):
+            return (POOL_TOKENS_UNIT0, POOL_TOKENS_UNIT1, POOL_TOKENS_LATER)[min(unit, 2)]
+
+        def gain_on_pool(unit):
+            split = pool_tokens(unit)
+            m_inter[unit] = work.tile([P, CHUNK, PACK], BF16, name="m_inter", bufs=1, align_bytes=64)
             nc.gpsimd.tensor_tensor(
-                out=mb[u][:, :split, :],
-                in0=ge[u][:, :, :split].rearrange("p t n -> p n t"),
-                in1=half_gain[:, h, :].unsqueeze(1).to_broadcast([P, split, PACK]),
+                out=m_inter[unit][:, :split, :],
+                in0=gelu_out[unit][:, :, :split].rearrange("p t n -> p n t"),
+                in1=half_gain[:, unit % G, :].unsqueeze(1).to_broadcast([P, split, PACK]),
                 op=ALU.mult)
 
-        def gain_vector(u):
-            h = u % G
-            split = POOL_TOKENS[min(u, 2)]
+        def gain_on_vector(unit):
+            split = pool_tokens(unit)
             nc.vector.tensor_tensor(
-                out=mb[u][:, split:, :].rearrange("p (c i) t -> p c t i", i=2),
-                in0=ge[u][:, :, split:].rearrange("p t (c i) -> p c t i", i=2),
-                in1=gain_bank[:, h, :].unsqueeze(1).unsqueeze(3).to_broadcast([P, (CHUNK - split) // 2, PACK, 2]),
+                out=m_inter[unit][:, split:, :].rearrange("p (c i) t -> p c t i", i=2),
+                in0=gelu_out[unit][:, :, split:].rearrange("p t (c i) -> p c t i", i=2),
+                in1=gain_bank[:, unit % G, :].unsqueeze(1).unsqueeze(3).to_broadcast([P, (CHUNK - split) // 2, PACK, 2]),
                 op=ALU.mult)
 
-        def quant_m(u):
-            mq[u] = quantize(mb[u][:].rearrange("p n t -> p (n t)"), "mq", work, "mq")
+        def quant_m(unit):
+            m_mx[unit] = quantize(m_inter[unit][:].rearrange("p n t -> p (n t)"), work, "m_mx", 3)
 
-        def gate_tanh(u, half):
-            c, h = divmod(u, G)
-            th[(u, half)] = work.tile([P, 2 * G, P], F32, name="gate_tanh", tag="gate_tanh%d" % half, bufs=3 - half)
-            src = gate[(c, half)][:].rearrange("p a (g h i) -> p (a g) h i", g=G, h=G)
-            nc.scalar.activation(out=th[(u, half)][:], in_=src[:, :, h, :], func=ACT.Tanh, scale=0.5, bias=zero_bias[:])
+        def tanh_gate(unit, pair):
+            chunk, h = divmod(unit, G)
+            gate_tanh[(unit, pair)] = work.tile([P, 2 * G, P], F32, name="gate_tanh%d" % pair, bufs=3 - pair)
+            src = gate_in[(chunk, pair)][:].rearrange("p a (g h j) -> p (a g) h j", g=G, h=G)
+            nc.scalar.activation(out=gate_tanh[(unit, pair)][:], in_=src[:, :, h, :], func=ACT.Tanh, scale=0.5, bias=zero_bias[:])
 
-        def right(u, a):
-            h = u % G
-            bank = psum.tile([P, S], F32, name="bank_v", tag="to_vector", bufs=4)
-            mc, ms = mq[u]
-            rc, rs = wq[("r", h)]
-            nc.tensor.matmul_mx(out=bank[:], lhsT=mc[:, a * P:(a + 1) * P].bitcast(FP8X4), lhsT_scale=ms[:, a * P:(a + 1) * P],
-                                rhs=rc[:].bitcast(FP8X4), rhs_scale=rs[:], start=True, stop=True)
-            acc2[(u, a)] = bank
+        def right(unit, a):
+            v_banks[(unit, a)] = psum.tile([P, S], F32, name="bank_v", tag="to_vector", bufs=VECTOR_BANKS)
+            mx_product(v_banks[(unit, a)], m_mx[unit], a * P, w_mx[("r", unit % G)])
 
-        def finish(u, a):
-            c, h = divmod(u, G)
-            res = work.tile([P, G, P], F32, name="res", tag="res", bufs=6)
-            half, aa = divmod(a, 2)
-            nc.vector.scalar_tensor_tensor(out=res[:], in0=th[(u, half)][:, aa * G:(aa + 1) * G, :], scalar=1.0,
-                                           in1=acc2[(u, a)][:].rearrange("p (i g) -> p g i", g=G),
+        def finish(unit, a):
+            chunk, h = divmod(unit, G)
+            pair, second = divmod(a, 2)
+            res = work.tile([P, G, P], F32, name="res", bufs=6)
+            nc.vector.scalar_tensor_tensor(out=res[:], in0=gate_tanh[(unit, pair)][:, second * G:(second + 1) * G, :], scalar=1.0,
+                                           in1=v_banks[(unit, a)][:].rearrange("p (j g) -> p g j", g=G),
                                            op0=ALU.add, op1=ALU.mult)
-            r0 = c * CHUNK + a * P
-            dst = out[r0:r0 + P, :].rearrange("p (g h i) -> p g h i", g=G, h=G)
+            row = chunk * CHUNK + a * P
+            dst = out[row:row + P, :].rearrange("p (g h j) -> p g h j", g=G, h=G)
             nc.sync.dma_start(out=dst[:, :, h, :], in_=res[:])
 
         widen_x(0, 0, D // 2)
         widen_x(0, D // 2, D)
         turn_x(0)
-        for i in range(1, TILES + 1):
-            if i < TILES:
-                weave_pool("l", i - 1)
-            widen_x(i, 0, D)
-            if i == TILES:
-                weave_pe("l", 3, 0)
-                weave_pe("l", 3, 1)
-            turn_x(i)
-            scale_x(i - 1)
-        widen_x(5, 0, D)
-        widen_x(6, 0, D)
-        gate_tanh(0, 0)
+        for tile in range(1, TILES + 1):
+            if tile < G:
+                interleave_on_pool("l", tile - 1)
+            widen_x(tile)
+            turn_x(tile)
+            scale_x(tile - 1)
+        interleave_on_scalar("l", G - 1)
+        widen_x(5)
+        turn_x(5)
+        widen_x(6)
+        tanh_gate(0, 0)
+        tanh_gate(1, 0)
         for g in range(G):
             quant_w("l", g)
             if g == 0:
@@ -229,55 +238,55 @@ def tile_monarchgatedmixer_kernel(tc, x_bytes, x_scale, t, lblk, rblk, kern, b, 
                 nc.vector.tensor_scalar(out=half_gain[:], in0=chan16[:, 2], scalar1=0.5, scalar2=None, op0=ALU.mult)
             quant_x(0, g)
             left(0, g)
-            if g < 2:
-                weave_pe("r", 0, g)
-        gain_pool(0)
-        turn_x(5)
+
+        gain_on_pool(0)
         scale_x(4)
-        for g in range(G):
-            left(1, g)
-        nc.tensor.matmul(gain_bank[:], lhsT=ident16[:], rhs=half_gain[:], start=True, stop=True)
-        widen_x(7, 0, D)
+        left(1, 0)
+        left(1, 1)
         turn_x(6)
+        widen_x(7)
+        left(1, 2)
+        left(1, 3)
         scale_x(5)
-        gate_tanh(0, 1)
+        interleave_on_tensor("r", 0)
+        tanh_gate(0, 1)
+        nc.tensor.matmul(gain_bank[:], lhsT=ident16[:], rhs=half_gain[:], start=True, stop=True)
         turn_x(7)
         scale_x(6)
-        gate_tanh(1, 0)
-        weave_pe("r", 1, 0)
-        weave_pe("r", 1, 1)
         quant_w("r", 0)
         quant_m(0)
         scale_x(7)
-        for u in range(UNITS):
-            if u + 1 < UNITS:
-                gain_pool(u + 1)
-            if u + 2 < UNITS:
-                for g in range(G - 1):
-                    left(u + 2, g)
-            right(u, 0)
-            right(u, 1)
-            if u + 2 < UNITS:
-                left(u + 2, G - 1)
-            if u + 1 < UNITS:
-                gate_tanh(u + 1, 1)
-            if u + 2 < UNITS:
-                gate_tanh(u + 2, 0)
-            if u + 2 < G:
-                weave_pe("r", u + 2, 0)
-                weave_pe("r", u + 2, 1)
-            right(u, 2)
-            right(u, 3)
-            if u + 1 < UNITS:
-                gain_vector(u + 1)
-            finish(u, 0)
-            finish(u, 1)
-            if u == 0:
+
+        for unit in range(UNITS):
+            if unit + 1 < UNITS:
+                gain_on_pool(unit + 1)
+            if unit + 2 < UNITS:
+                for g in range(SCALAR_BANKS):
+                    left(unit + 2, g)
+            right(unit, 0)
+            right(unit, 1)
+            if unit + 2 < UNITS:
+                left(unit + 2, G - 1)
+            if unit == 0:
+                interleave_on_tensor("r", 1)
+            if unit + 1 < UNITS:
+                tanh_gate(unit + 1, 1)
+            right(unit, 2)
+            right(unit, 3)
+            if unit + 2 < G:
+                interleave_on_tensor("r", unit + 2)
+            if unit + 2 < UNITS:
+                tanh_gate(unit + 2, 0)
+            if unit + 1 < UNITS:
+                gain_on_vector(unit + 1)
+            finish(unit, 0)
+            finish(unit, 1)
+            if unit == 0:
                 for g in range(G):
                     quant_x(1, g)
-            if u + 1 < G:
-                quant_w("r", u + 1)
-            if u + 1 < UNITS:
-                quant_m(u + 1)
-            finish(u, 2)
-            finish(u, 3)
+            if unit + 1 < G:
+                quant_w("r", unit + 1)
+            if unit + 1 < UNITS:
+                quant_m(unit + 1)
+            finish(unit, 2)
+            finish(unit, 3)

from contextlib import ExitStack

import concourse.mybir as mybir
from concourse.masks import make_identity

N, G, S = 1024, 4, 512
D = G * S
FLOPS = 2 * 2 * N * G * S * S

F32 = mybir.dt.float32
BF16 = mybir.dt.bfloat16
U32 = mybir.dt.uint32
U8 = mybir.dt.uint8
FP8 = mybir.dt.float8_e4m3fn
FP8X4 = mybir.dt.float8_e4m3fn_x4
ACT = mybir.ActivationFunctionType
ALU = mybir.AluOpType

P = 128
PACK = 4
CHUNK = 512
TILES = CHUNK // P
UNITS = (N // CHUNK) * G
GROUP_WORDS = S // 2

POOL_TOKENS_UNIT0, POOL_TOKENS_UNIT1, POOL_TOKENS_LATER = 512, 384, 256

VECTOR_BANKS, SCALAR_BANKS = 4, 3


def tile_monarchgatedmixer_kernel(tc, x_bytes, x_scale, t, lblk, rblk, kern, b, gain, out):
    nc = tc.nc
    with ExitStack() as ctx:
        keep = ctx.enter_context(tc.tile_pool(name="keep", bufs=1))
        work = ctx.enter_context(tc.tile_pool(name="work", bufs=2))
        psum = ctx.enter_context(tc.psum_pool(name="psum", bufs=1))
        ctx.enter_context(tc.manual_schedule())

        zero_in = keep.tile([P, 1], F32, name="zero_in")
        zero_bias = keep.tile([P, 1], F32, name="zero_bias")
        nc.vector.memset(zero_in[:], 0.0)
        nc.scalar.activation(out=zero_bias[:], in_=zero_in[:], func=ACT.Gelu_apprx_tanh)
        ident32 = keep.tile([P, P], F32, name="ident32")
        make_identity(nc, ident32[:])
        ident16 = keep.tile([P, P], BF16, name="ident16")
        make_identity(nc, ident16[:])

        xbytes, w_raw, gate_in = {}, {}, {}

        def load_x(tile):
            xbytes[tile] = keep.tile([P, D], U8, name="xbytes%d" % tile)
            nc.sync.dma_start(out=xbytes[tile][:], in_=x_bytes[tile * P:(tile + 1) * P, :])

        def load_w(side, src, g):
            w_raw[(side, g)] = keep.tile([P, PACK, S], BF16, name="raw_%s%d" % (side, g))
            nc.sync.dma_start(out=w_raw[(side, g)][:], in_=src[g].rearrange("(p t) j -> p t j", t=PACK))

        def load_t(chunk, pair):
            gate_in[(chunk, pair)] = keep.tile([P, 2, D], BF16, name="gate_in%d%d" % (chunk, pair))
            row = chunk * CHUNK + pair * 2 * P
            nc.sync.dma_start(out=gate_in[(chunk, pair)][:], in_=t[row:row + 2 * P, :].rearrange("(a p) d -> p a d", p=P))

        scale_col = keep.tile([P, G, PACK], F32, name="scale_col")
        chan16 = keep.tile([P, 3, G, PACK], BF16, name="chan16")
        load_x(0)
        nc.sync.dma_start(out=scale_col[:], in_=x_scale.rearrange("o (g p t) -> p (o g) t", p=P, t=PACK))
        for g in range(G - 1):
            load_w("l", lblk, g)
            load_x(g + 1)
        load_x(4)
        load_w("l", lblk, G - 1)
        for i, src in enumerate((kern, b, gain)):
            nc.sync.dma_start(out=chan16[:, i], in_=src.rearrange("h (p t) -> p h t", t=PACK))
        load_x(5)
        load_x(6)
        load_t(0, 0)
        load_w("r", rblk, 0)
        load_x(7)
        load_t(0, 1)
        load_w("r", rblk, 1)
        load_w("r", rblk, 2)
        load_t(1, 0)
        load_w("r", rblk, 3)
        load_t(1, 1)

        affine = keep.tile([P, 2, G * PACK], F32, name="affine")
        half_gain = keep.tile([P, G, PACK], BF16, name="half_gain")
        gain_bank = psum.tile([P, G, PACK], F32, name="gain_bank")

        x_wide, x_banks, x_inter, x_mx = {}, {}, {}, {}
        w_inter, w_mx = {}, {}
        gelu_out, m_inter, m_mx, gate_tanh, v_banks = {}, {}, {}, {}, {}

        def quantize(src, pool, name, bufs):
            codes = pool.tile([P, S], U32, name=name + "_codes", align_bytes=64, bufs=bufs)
            scales = pool.tile([P, S], U8, name=name + "_scales", align_bytes=64, bufs=bufs)
            nc.vector.quantize_mx(out=codes[:].bitcast(FP8X4), scales=scales[:], in_=src)
            return codes, scales

        def mx_product(bank, stationary, first_col, moving):
            cols = slice(first_col, first_col + P)
            nc.tensor.matmul_mx(out=bank[:], lhsT=stationary[0][:, cols].bitcast(FP8X4), lhsT_scale=stationary[1][:, cols],
                                rhs=moving[0][:].bitcast(FP8X4), rhs_scale=moving[1][:], start=True, stop=True)

        def widen_x(tile, lo=0, hi=D):
            if lo == 0:
                x_wide[tile] = work.tile([P, D], BF16, name="x_wide", bufs=3)
            nc.scalar.copy(out=x_wide[tile][:, lo:hi], in_=xbytes[tile][:, lo:hi].bitcast(FP8))

        def turn_x(tile):
            words = x_wide[tile][:].bitcast(F32)
            for g0 in (0, 2):
                bank = psum.tile([P, 2, 2, P], F32, name="bank_x", tag="to_vector", bufs=VECTOR_BANKS)
                for dg in range(2):
                    w0 = GROUP_WORDS * (g0 + dg)
                    for u in range(2):
                        nc.tensor.transpose(bank[:, u, dg, :], words[:, w0 + u:w0 + GROUP_WORDS:2], ident32[:])
                x_banks[(tile, g0)] = bank

        def scale_x(tile):
            chunk, a = divmod(tile, TILES)
            if a == 0:
                x_inter[chunk] = work.tile([P, G, CHUNK, 2, 2], BF16, name="x_inter", bufs=1, align_bytes=64)
            for g0 in (0, 2):
                values = x_banks[(tile, g0)][:].rearrange("p u g n -> p (u g n)").bitcast(BF16)
                scales = scale_col[:, g0:g0 + 2, :].rearrange("p g (u e) -> p g u e", u=2)
                nc.vector.tensor_tensor(
                    out=x_inter[chunk][:, g0:g0 + 2, a * P:(a + 1) * P],
                    in0=values.rearrange("p (u g n e) -> p g n u e", u=2, g=2, e=2),
                    in1=scales.unsqueeze(2).to_broadcast([P, 2, P, 2, 2]),
                    op=ALU.mult)

        def quant_x(chunk, g):
            src = x_inter[chunk][:, g].rearrange("p n u e -> p (n u e)")
            x_mx[(chunk, g)] = quantize(src, keep, "x_mx%d%d" % (chunk, g), 1)

        def new_w_inter(side, g):
            w_inter[(side, g)] = work.tile([P, S * PACK], BF16, name="w_inter", bufs=G, align_bytes=64)
            return w_inter[(side, g)]

        def interleave_on_pool(side, g):
            nc.gpsimd.tensor_scalar(out=new_w_inter(side, g)[:].rearrange("p (j t) -> p j t", t=PACK),
                                    in0=w_raw[(side, g)][:].rearrange("p t j -> p j t"),
                                    scalar1=1.0, scalar2=0.0, op0=ALU.mult, op1=ALU.add)

        def interleave_on_scalar(side, g):
            nc.scalar.copy(out=new_w_inter(side, g)[:].rearrange("p (c i t) -> p c t i", i=4, t=PACK),
                           in_=w_raw[(side, g)][:].rearrange("p t (c i) -> p c t i", i=4))

        def interleave_on_tensor(side, g):
            dst = new_w_inter(side, g)
            for half in range(2):
                bank = psum.tile([P, 2, P, PACK], BF16, name="bank_w", tag="to_scalar", bufs=SCALAR_BANKS)
                for q in range(2):
                    j0 = (2 * half + q) * P
                    nc.tensor.matmul(bank[:, q], lhsT=ident16[:],
                                     rhs=w_raw[(side, g)][:, :, j0:j0 + P].rearrange("p t j -> p j t"),
                                     start=True, stop=True)
                width = 2 * P * PACK
                nc.scalar.copy(out=dst[:, width * half:width * (half + 1)], in_=bank[:].rearrange("p q j t -> p (q j t)"))

        def quant_w(side, g):
            w_mx[(side, g)] = quantize(w_inter[(side, g)][:], keep, "w_mx_%s%d" % (side, g), 1)

        def left(unit, g):
            chunk, h = divmod(unit, G)
            if g == 0:
                gelu_out[unit] = work.tile([P, PACK, CHUNK], F32, name="gelu_out", bufs=3)
            bank = psum.tile([P, CHUNK], F32, name="bank_u", tag="to_scalar", bufs=SCALAR_BANKS)
            mx_product(bank, w_mx[("l", g)], h * P, x_mx[(chunk, g)])
            col = h * PACK + g
            nc.scalar.activation(out=gelu_out[unit][:, g, :], in_=bank[:], func=ACT.Gelu_apprx_tanh,
                                 scale=affine[:, 0, col:col + 1], bias=affine[:, 1, col:col + 1])

        def pool_tokens(unit):
            return (POOL_TOKENS_UNIT0, POOL_TOKENS_UNIT1, POOL_TOKENS_LATER)[min(unit, 2)]

        def gain_on_pool(unit):
            split = pool_tokens(unit)
            m_inter[unit] = work.tile([P, CHUNK, PACK], BF16, name="m_inter", bufs=1, align_bytes=64)
            nc.gpsimd.tensor_tensor(
                out=m_inter[unit][:, :split, :],
                in0=gelu_out[unit][:, :, :split].rearrange("p t n -> p n t"),
                in1=half_gain[:, unit % G, :].unsqueeze(1).to_broadcast([P, split, PACK]),
                op=ALU.mult)

        def gain_on_vector(unit):
            split = pool_tokens(unit)
            nc.vector.tensor_tensor(
                out=m_inter[unit][:, split:, :].rearrange("p (c i) t -> p c t i", i=2),
                in0=gelu_out[unit][:, :, split:].rearrange("p t (c i) -> p c t i", i=2),
                in1=gain_bank[:, unit % G, :].unsqueeze(1).unsqueeze(3).to_broadcast([P, (CHUNK - split) // 2, PACK, 2]),
                op=ALU.mult)

        def quant_m(unit):
            m_mx[unit] = quantize(m_inter[unit][:].rearrange("p n t -> p (n t)"), work, "m_mx", 3)

        def tanh_gate(unit, pair):
            chunk, h = divmod(unit, G)
            gate_tanh[(unit, pair)] = work.tile([P, 2 * G, P], F32, name="gate_tanh%d" % pair, bufs=3 - pair)
            src = gate_in[(chunk, pair)][:].rearrange("p a (g h j) -> p (a g) h j", g=G, h=G)
            nc.scalar.activation(out=gate_tanh[(unit, pair)][:], in_=src[:, :, h, :], func=ACT.Tanh, scale=0.5, bias=zero_bias[:])

        def right(unit, a):
            v_banks[(unit, a)] = psum.tile([P, S], F32, name="bank_v", tag="to_vector", bufs=VECTOR_BANKS)
            mx_product(v_banks[(unit, a)], m_mx[unit], a * P, w_mx[("r", unit % G)])

        def finish(unit, a):
            chunk, h = divmod(unit, G)
            pair, second = divmod(a, 2)
            res = work.tile([P, G, P], F32, name="res", bufs=6)
            nc.vector.scalar_tensor_tensor(out=res[:], in0=gate_tanh[(unit, pair)][:, second * G:(second + 1) * G, :], scalar=1.0,
                                           in1=v_banks[(unit, a)][:].rearrange("p (j g) -> p g j", g=G),
                                           op0=ALU.add, op1=ALU.mult)
            row = chunk * CHUNK + a * P
            dst = out[row:row + P, :].rearrange("p (g h j) -> p g h j", g=G, h=G)
            nc.sync.dma_start(out=dst[:, :, h, :], in_=res[:])

        widen_x(0, 0, D // 2)
        widen_x(0, D // 2, D)
        turn_x(0)
        for tile in range(1, TILES + 1):
            if tile < G:
                interleave_on_pool("l", tile - 1)
            widen_x(tile)
            turn_x(tile)
            scale_x(tile - 1)
        interleave_on_scalar("l", G - 1)
        widen_x(5)
        turn_x(5)
        widen_x(6)
        tanh_gate(0, 0)
        tanh_gate(1, 0)
        for g in range(G):
            quant_w("l", g)
            if g == 0:
                nc.vector.tensor_copy(out=affine[:], in_=chan16[:, 0:2].rearrange("p i h t -> p i (h t)"))
                nc.vector.tensor_scalar(out=half_gain[:], in0=chan16[:, 2], scalar1=0.5, scalar2=None, op0=ALU.mult)
            quant_x(0, g)
            left(0, g)

        gain_on_pool(0)
        scale_x(4)
        left(1, 0)
        left(1, 1)
        turn_x(6)
        widen_x(7)
        left(1, 2)
        left(1, 3)
        scale_x(5)
        interleave_on_tensor("r", 0)
        tanh_gate(0, 1)
        nc.tensor.matmul(gain_bank[:], lhsT=ident16[:], rhs=half_gain[:], start=True, stop=True)
        turn_x(7)
        scale_x(6)
        quant_w("r", 0)
        quant_m(0)
        scale_x(7)

        for unit in range(UNITS):
            if unit + 1 < UNITS:
                gain_on_pool(unit + 1)
            if unit + 2 < UNITS:
                for g in range(SCALAR_BANKS):
                    left(unit + 2, g)
            right(unit, 0)
            right(unit, 1)
            if unit + 2 < UNITS:
                left(unit + 2, G - 1)
            if unit == 0:
                interleave_on_tensor("r", 1)
            if unit + 1 < UNITS:
                tanh_gate(unit + 1, 1)
            right(unit, 2)
            right(unit, 3)
            if unit + 2 < G:
                interleave_on_tensor("r", unit + 2)
            if unit + 2 < UNITS:
                tanh_gate(unit + 2, 0)
            if unit + 1 < UNITS:
                gain_on_vector(unit + 1)
            finish(unit, 0)
            finish(unit, 1)
            if unit == 0:
                for g in range(G):
                    quant_x(1, g)
            if unit + 1 < G:
                quant_w("r", unit + 1)
            if unit + 1 < UNITS:
                quant_m(unit + 1)
            finish(unit, 2)
            finish(unit, 3)
